import numpy as np
import ml_dtypes


def mxq(x, axis, fmt="e4m3"):
    dtype, down = {"e4m3": (ml_dtypes.float8_e4m3fn, 7), "e5m2": (ml_dtypes.float8_e5m2, 14)}[fmt]
    v = np.moveaxis(np.asarray(x, np.float32).astype(ml_dtypes.bfloat16).astype(np.float64), axis, -1)
    blocks = v.reshape(v.shape[:-1] + (-1, 32))
    amax = np.abs(blocks).max(-1, keepdims=True)
    byte = np.maximum(np.where(amax > 0, np.frexp(amax)[1] - 1 + 127, 0) - down, 1)
    scale = np.exp2(byte - 127.0)
    codes = (blocks / scale).astype(np.float32).astype(dtype).astype(np.float64)
    return np.moveaxis((codes * scale).reshape(v.shape), -1, axis)


WIDE = False


def mx_kscale(k):
    if not WIDE:
        return np.ones(k)
    levels = np.array([10, -10, 5, -5, 0])
    if k % 512:
        return np.exp2(np.random.permutation(np.resize(levels, k // 32))).repeat(32)
    a = np.empty((k // 512, 16))
    for p in range(k // 512):
        a[p, :8] = np.random.permutation(np.resize(levels, 8))
        for g in range(8):
            far = levels[np.abs(levels - a[p, g]) >= 10]
            a[p, g + 8] = far[np.random.randint(len(far))]
    return np.exp2(a.ravel()).repeat(32)


def f64(x):
    return np.asarray(x).astype(np.float64)


def striped(idx):
    return np.tile(np.asarray(idx).reshape(-1, 16).T, (8, 1)).astype(np.uint16)


def unstriped(offs):
    return offs[:16].T.reshape(-1).astype(np.int64)


E2M1 = np.array([0.0, 0.5, 1.0, 1.5, 2.0, 3.0, 4.0, 6.0, -0.0, -0.5, -1.0, -1.5, -2.0, -3.0, -4.0, -6.0])


def pack_weight(w, fmt):
    k, n = w.shape
    w = f64(np.asarray(w, np.float32).astype(ml_dtypes.bfloat16)).reshape(k // 32, 32, n)
    amax = np.abs(w).max(1)
    if fmt == "e4m3":
        byte = np.frexp(amax)[1] - 1 + 127 - 7
    else:
        mant, ex = np.frexp(amax / 6.0)
        byte = np.where(mant > 0.5, ex, ex - 1) + 127
    byte = np.clip(np.where(amax > 0, byte, 1), 1, 254)
    scaled = (w * np.exp2(127.0 - byte)[:, None, :]).reshape(k, n).astype(np.float32)
    by_word = np.ascontiguousarray(scaled.reshape(k // 512, 128, 4, n).transpose(0, 1, 3, 2))
    if fmt == "e4m3":
        words = by_word.astype(ml_dtypes.float8_e4m3fn).view(np.uint8)
    else:
        c = by_word.astype(ml_dtypes.float4_e2m1fn).view(np.uint8) & 0xF
        words = (c[..., 0::2] | (c[..., 1::2] << 4)).reshape(k // 512, 128, 2 * n)
    return np.ascontiguousarray(words), np.ascontiguousarray(byte.astype(np.uint8).reshape(k // 512, 16, n))


def unpack_weight(words, scales, fmt):
    g, _, n = scales.shape
    words = np.ascontiguousarray(words).reshape(g, 128, n, -1)
    if fmt == "e4m3":
        vals = words.view(ml_dtypes.float8_e4m3fn).astype(np.float64)
    else:
        nib = np.empty((g, 128, n, 4), np.uint8)
        nib[..., 0::2] = words & 0xF
        nib[..., 1::2] = words >> 4
        vals = E2M1[nib]
    vals = vals * np.repeat(np.exp2(scales.astype(np.float64) - 127.0), 8, axis=1)[..., None]
    return vals.transpose(0, 1, 3, 2).reshape(g * 512, n)


def sigmoid(v):
    return 1.0 / (1.0 + np.exp(-v))


D, K, R, T, I, Q = 512, 512, 512, 2048, 512, 128


def setup_inputs():
    n = np.random.standard_normal
    idx = np.random.permutation(T)[:I]
    fd = mx_kscale(D)
    fk = mx_kscale(K)
    fr = mx_kscale(R)
    keysp = pack_weight(n((D, T)) / fd[:, None], "e2m1")
    tabp = pack_weight(n((K, T)) / fk[:, None], "e2m1")
    return {
        "query": (n((D, Q)) * 0.6 / np.sqrt(D) * fd[:, None]).astype(np.float32),
        "query2": (n((D, Q)) * 1.0 / np.sqrt(D) * fd[:, None]).astype(np.float32),
        "keys_words": keysp[0],
        "keys_scales": keysp[1],
        "tab_words": tabp[0],
        "tab_scales": tabp[1],
        "w1": (n((K, R)) * 1 / np.sqrt(K) * fk[:, None]).astype(np.float32),
        "gain": (np.random.uniform(0.5, 2.0, (R, 1))).astype(np.float32),
        "gout": (n((R, Q)) * 1 / np.sqrt(R) * fr[:, None]).astype(np.float32),
        "hsc": (np.random.uniform(0.7, 1.4, (R, 1)) / fr[:, None]).astype(np.float32),
        "old": (0.5 * n((Q, T))).astype(np.float32),
        "offs": striped(idx),
    }


def reference(query, query2, keys_words, keys_scales, tab_words, tab_scales, w1, gain, gout, hsc, old, offs):
    idx = unstriped(offs)
    keysu = unpack_weight(keys_words, keys_scales, "e2m1")
    tabu = unpack_weight(tab_words, tab_scales, "e2m1")
    queryq = mxq(f64(query), 0, "e4m3")
    keysidxg = keysu[:, idx]
    a = queryq.T @ keysidxg
    query2q = mxq(f64(query2), 0, "e4m3")
    b = query2q.T @ keysidxg
    p = np.exp(a - np.max(a, axis=1, keepdims=True)) * sigmoid(b)
    z = np.sum(p, axis=1, keepdims=True)
    w1q = mxq(f64(w1), 0, "e4m3")
    tabidxg = tabu[:, idx]
    zh = w1q.T @ tabidxg
    ht = np.tanh(zh)
    hv = ht * f64(gain)
    hs1 = hv * f64(hsc)
    goutq = mxq(f64(gout), 0, "e4m3")
    hs1q = mxq(hs1, 0, "e4m3")
    c0 = goutq.T @ hs1q
    dz = np.sum(c0 * p / np.square(z) * (-1.0), axis=1, keepdims=True)
    dp = c0 / z + dz
    da = dp * sigmoid(b) * np.exp(a - np.max(a, axis=1, keepdims=True))
    gs = da * 512.0
    gf = np.zeros((Q, T))
    gf[:, idx] = gs
    y = f64(old) + gf
    return y

@@ -1,0 +1,240 @@
+from contextlib import ExitStack
+
+import concourse.mybir as mybir
+
+D, K, R, T, I, Q = 512, 512, 512, 2048, 512, 128
+FLOPS = 2 * (2 * D * Q * I + K * R * I + R * Q * I)
+
+F32 = mybir.dt.float32
+BF16 = mybir.dt.bfloat16
+I32 = mybir.dt.int32
+U32 = mybir.dt.uint32
+U16 = mybir.dt.uint16
+U8 = mybir.dt.uint8
+FP8X4 = mybir.dt.float8_e4m3fn_x4
+FP4X4 = mybir.dt.float4_e2m1fn_x4
+ALU = mybir.AluOpType
+ACT = mybir.ActivationFunctionType
+
+P = 128
+PACK = 4
+CHUNK = 128
+HALF_COLS = R // 2
+STORE_WIDTHS = (512, 512, 512, 256, 256)
+
+
+def load_scale_rows(queue, plane, rows):
+    for quad in range(4):
+        queue.dma_start(
+            out=plane[32 * quad : 32 * quad + 4, :].bitcast(I32),
+            in_=rows[0, 4 * quad : 4 * quad + 4, :].bitcast(I32),
+        )
+
+
+def tile_attend_blrgained_asked_kernel(
+    tc, query, query2, keys_words, keys_scales, tab_words, tab_scales, w1, gain, gout, hsc, old, offs, out
+):
+    nc = tc.nc
+    with ExitStack() as ctx:
+        sb = ctx.enter_context(tc.tile_pool(name="sb", bufs=1))
+        ps = ctx.enter_context(tc.psum_pool(name="ps", bufs=1))
+
+        offsets = sb.tile([P, I // 16], U16, name="offsets")
+        tab_plane = sb.tile([P, T], U8, name="tab_plane", align_bytes=64)
+        keys_plane = sb.tile([P, T], U8, name="keys_plane", align_bytes=64)
+        tab_pool = sb.tile([P, T], U16, name="tab_pool", align_bytes=64)
+        keys_pool = sb.tile([P, T], U16, name="keys_pool", align_bytes=64)
+        placed = sb.tile([P, T], F32, name="placed", align_bytes=64)
+        total = sb.tile([P, T], F32, name="total", align_bytes=64)
+        w_raw = [sb.tile([P, PACK, HALF_COLS], F32, name=f"w_raw{h}", tag=f"w_raw{h}", align_bytes=64) for h in range(2)]
+        q_raw = sb.tile([P, PACK, Q], F32, name="q_raw", align_bytes=64)
+        q2_raw = sb.tile([P, PACK, Q], F32, name="q2_raw", align_bytes=64)
+        gout_raw = sb.tile([P, PACK, Q], F32, name="gout_raw", align_bytes=64)
+        gain_sb = sb.tile([P, PACK], F32, name="gain_sb")
+        hsc_sb = sb.tile([P, PACK], F32, name="hsc_sb")
+
+        nc.vector.memset(keys_plane[:].bitcast(I32), 0)
+        nc.vector.memset(tab_plane[:].bitcast(I32), 0)
+
+        w_rows = w1.rearrange("(p j) c -> p j c", j=PACK)
+        nc.sync.dma_start(offsets[:], offs)
+        load_scale_rows(nc.scalar, keys_plane, keys_scales)
+        nc.sync.dma_start(out=q_raw[:], in_=query.rearrange("(p j) c -> p j c", j=PACK))
+        nc.sync.dma_start(out=keys_pool[:].bitcast(I32), in_=keys_words[0].bitcast(I32))
+        nc.sync.dma_start(out=q2_raw[:], in_=query2.rearrange("(p j) c -> p j c", j=PACK))
+        nc.sync.dma_start(out=gout_raw[:], in_=gout.rearrange("(p j) c -> p j c", j=PACK))
+        nc.sync.dma_start(out=w_raw[0][:], in_=w_rows[:, :, 0:HALF_COLS])
+        load_scale_rows(nc.sync, tab_plane, tab_scales)
+        nc.sync.dma_start(out=w_raw[1][:], in_=w_rows[:, :, HALF_COLS:R])
+        nc.sync.dma_start(out=tab_pool[:].bitcast(I32), in_=tab_words[0].bitcast(I32))
+        nc.sync.dma_start(out=total[:], in_=old)
+        nc.gpsimd.dma_start(out=gain_sb[:], in_=gain.rearrange("(p t) o -> p (t o)", t=PACK))
+        nc.gpsimd.dma_start(out=hsc_sb[:], in_=hsc.rearrange("(p t) o -> p (t o)", t=PACK))
+
+        nc.gpsimd.memset(placed[:], 0.0)
+        factor = sb.tile([P, PACK], F32, name="factor")
+        nc.gpsimd.tensor_tensor(factor[:], gain_sb[:], hsc_sb[:], ALU.mult)
+
+        tab_bytes = sb.tile([P, I], U8, name="tab_bytes", align_bytes=64)
+        keys_bytes = sb.tile([P, I], U8, name="keys_bytes", align_bytes=64)
+        tab_codes = sb.tile([P, I], U16, name="tab_codes", align_bytes=64)
+        keys_codes = sb.tile([P, I], U16, name="keys_codes", align_bytes=64)
+        w_codes = sb.tile([P, PACK, P], U32, name="w_codes", align_bytes=64)
+        w_bytes = sb.tile([P, PACK, P], U8, name="w_bytes", align_bytes=64)
+
+        def cast_w(h):
+            grouped = sb.tile([P, PACK, P // 2, PACK], BF16, name=f"w_grouped{h}", align_bytes=64)
+            nc.scalar.activation(
+                grouped[:].rearrange("p t m j -> p m j t"),
+                w_raw[h][:].rearrange("p j (m t) -> p m j t", t=PACK),
+                ACT.Copy,
+            )
+            return grouped
+
+        def quantize_w(h, grouped):
+            cols = slice(h * P // 2, (h + 1) * P // 2)
+            for t in range(PACK):
+                nc.vector.quantize_mx(
+                    out=w_codes[:, t, cols].bitcast(FP8X4),
+                    scales=w_bytes[:, t, cols],
+                    in_=grouped[:, t].rearrange("p m j -> p (m j)"),
+                )
+
+        def cast_cols(raw, name):
+            grouped = sb.tile([P, Q, PACK], BF16, name=name + "_grouped", align_bytes=64)
+            nc.scalar.activation(
+                grouped[:].rearrange("p (c i) j -> p c j i", i=4),
+                raw[:].rearrange("p j (c i) -> p c j i", i=4),
+                ACT.Copy,
+            )
+            return grouped
+
+        def quantize_cols(grouped, name):
+            codes = sb.tile([P, Q], U32, name=name + "_codes", align_bytes=64)
+            scales = sb.tile([P, Q], U8, name=name + "_bytes", align_bytes=64)
+            nc.vector.quantize_mx(
+                out=codes[:].bitcast(FP8X4), scales=scales[:], in_=grouped[:].rearrange("p c j -> p (c j)")
+            )
+            return codes, scales
+
+        n_chunks = I // CHUNK
+        zh = [ps.tile([P, PACK, CHUNK], F32, name=f"zh{c}") for c in range(n_chunks)]
+        a_ps = ps.tile([P, I], F32, name="a_ps")
+        b_ps = ps.tile([P, I], F32, name="b_ps")
+        c0_ps = ps.tile([P, I], F32, name="c0_ps")
+
+        def gather_tab(h):
+            nc.vector.tensor_copy(
+                tab_codes[:, h * I // 2 : (h + 1) * I // 2], tab_pool[:].indirect(offsets[:, h * 16 : (h + 1) * 16])
+            )
+
+        def layer(c):
+            cols = slice(c * CHUNK, (c + 1) * CHUNK)
+            for t in range(PACK):
+                nc.tensor.matmul_mx(
+                    out=zh[c][:, t, :],
+                    lhsT=w_codes[:, t, :].bitcast(FP8X4),
+                    lhsT_scale=w_bytes[:, t, :],
+                    rhs=tab_codes[:, cols].bitcast(FP4X4),
+                    rhs_scale=tab_bytes[:, cols],
+                    start=True,
+                    stop=True,
+                )
+
+        def squash(c):
+            ht = sb.tile([P, CHUNK, PACK], F32, name=f"ht{c}", align_bytes=64)
+            nc.scalar.activation(ht[:], zh[c][:].rearrange("p t n -> p n t"), ACT.Tanh)
+            return ht
+
+        def scale_hidden(c, ht):
+            hs = sb.tile([P, CHUNK, PACK], BF16, name=f"hs{c}_grouped", align_bytes=64)
+            nc.vector.tensor_tensor(hs[:], ht[:], factor[:].unsqueeze(1).to_broadcast([P, CHUNK, PACK]), ALU.mult)
+            return hs
+
+        def scores(bank, codes, scales):
+            nc.tensor.matmul_mx(
+                out=bank[:],
+                lhsT=codes[:].bitcast(FP8X4),
+                lhsT_scale=scales[:],
+                rhs=keys_codes[:].bitcast(FP4X4),
+                rhs_scale=keys_bytes[:],
+                start=True,
+                stop=True,
+            )
+
+        nc.vector.tensor_copy(keys_bytes[:], keys_plane[:].indirect(offsets[:]))
+        q_grouped = cast_cols(q_raw, "q")
+        q2_grouped = cast_cols(q2_raw, "q2")
+        gout_grouped = cast_cols(gout_raw, "gout")
+        nc.vector.tensor_copy(keys_codes[:], keys_pool[:].indirect(offsets[:]))
+        q_codes, q_bytes = quantize_cols(q_grouped, "q")
+        q2_codes, q2_bytes = quantize_cols(q2_grouped, "q2")
+        scores(a_ps, q_codes, q_bytes)
+        scores(b_ps, q2_codes, q2_bytes)
+        gout_codes, gout_bytes = quantize_cols(gout_grouped, "gout")
+        nc.vector.tensor_copy(tab_bytes[:], tab_plane[:].indirect(offsets[:]))
+
+        w_grouped = [cast_w(h) for h in range(2)]
+        neg_a = sb.tile([P, I], F32, name="neg_a")
+        neg_max = sb.tile([P, 1], F32, name="neg_max")
+        nc.vector.tensor_scalar(neg_a[:], a_ps[:], -1.0, None, ALU.mult, ALU.min, accum_out=neg_max[:])
+        quantize_w(0, w_grouped[0])
+        logit = sb.tile([P, I], F32, name="logit")
+        nc.vector.scalar_tensor_tensor(logit[:], b_ps[:], 0.0, neg_a[:], ALU.min, ALU.subtract)
+        gather_tab(0)
+        quantize_w(1, w_grouped[1])
+        gather_tab(1)
+        for c in range(n_chunks):
+            layer(c)
+
+        half_abs = sb.tile([P, I], F32, name="half_abs", tag="w_raw1", align_bytes=64)
+        nc.scalar.activation(half_abs[:], b_ps[:], ACT.Abs, scale=0.5)
+        gate = sb.tile([P, I], F32, name="gate")
+        nc.scalar.activation(gate[:], half_abs[:], ACT.Tanh)
+        expo = sb.tile([P, I], F32, name="expo")
+        nc.scalar.activation(expo[:], logit[:], ACT.Exp, bias=neg_max[:])
+        ht = [squash(c) for c in range(n_chunks)]
+
+        weight = sb.tile([P, I], F32, name="weight")
+        row_sum = sb.tile([P, 1], F32, name="row_sum")
+        nc.vector.scalar_tensor_tensor(weight[:], gate[:], 1.0, expo[:], ALU.add, ALU.mult, accum_out=row_sum[:])
+        hs = [scale_hidden(0, ht[0])]
+        inv = sb.tile([P, 1], F32, name="inv")
+        nc.vector.reciprocal(inv[:], row_sum[:])
+        hs.append(scale_hidden(1, ht[1]))
+        inv_scaled = sb.tile([P, 1], F32, name="inv_scaled")
+        nc.vector.tensor_scalar(inv_scaled[:], inv[:], 512.0, None, ALU.mult)
+        neg_inv = sb.tile([P, 1], F32, name="neg_inv")
+        nc.vector.tensor_scalar(neg_inv[:], inv[:], -1.0, None, ALU.mult)
+        hq = [quantize_cols(hs[0], "hs0")]
+        for c in range(2, n_chunks):
+            hs.append(scale_hidden(c, ht[c]))
+            hq.append(quantize_cols(hs[c - 1], f"hs{c - 1}"))
+        hq.append(quantize_cols(hs[-1], f"hs{n_chunks - 1}"))
+
+        for c in range(n_chunks):
+            nc.tensor.matmul_mx(
+                out=c0_ps[:, c * CHUNK : (c + 1) * CHUNK],
+                lhsT=gout_codes[:].bitcast(FP8X4),
+                lhsT_scale=gout_bytes[:],
+                rhs=hq[c][0][:].bitcast(FP8X4),
+                rhs_scale=hq[c][1][:],
+                start=True,
+                stop=True,
+            )
+
+        direct = sb.tile([P, I], F32, name="direct")
+        direct_sum = sb.tile([P, 1], F32, name="direct_sum")
+        nc.vector.scalar_tensor_tensor(
+            direct[:], c0_ps[:], inv_scaled[:], weight[:], ALU.mult, ALU.mult, accum_out=direct_sum[:]
+        )
+        through = sb.tile([P, I], F32, name="through")
+        nc.vector.tensor_scalar(through[:], weight[:], direct_sum[:], neg_inv[:], ALU.mult, ALU.mult)
+        nc.vector.tensor_tensor(placed[:].indirect(offsets[:]), direct[:], through[:], ALU.add)
+
+        start = 0
+        for width in STORE_WIDTHS:
+            cols = slice(start, start + width)
+            nc.vector.tensor_tensor(total[:, cols], placed[:, cols], total[:, cols], ALU.add)
+            nc.sync.dma_start(out=out[:, cols], in_=total[:, cols])
+            start = start + width

@@ -20,7 +20,7 @@ P = 128
 PACK = 4
 CHUNK = 128
 HALF_COLS = R // 2
-STORE_WIDTHS = (512, 512, 512, 256, 256)
+STORE_WIDTHS = (256, 512, 512, 512, 256)
 
 
 def load_scale_rows(queue, plane, rows):
@@ -55,25 +55,22 @@ def tile_attend_blrgained_asked_kernel(
 
         nc.vector.memset(keys_plane[:].bitcast(I32), 0)
         nc.vector.memset(tab_plane[:].bitcast(I32), 0)
+        nc.vector.memset(placed[:], 0.0)
 
         w_rows = w1.rearrange("(p j) c -> p j c", j=PACK)
         nc.sync.dma_start(offsets[:], offs)
-        load_scale_rows(nc.scalar, keys_plane, keys_scales)
-        nc.sync.dma_start(out=q_raw[:], in_=query.rearrange("(p j) c -> p j c", j=PACK))
         nc.sync.dma_start(out=keys_pool[:].bitcast(I32), in_=keys_words[0].bitcast(I32))
+        load_scale_rows(nc.sync, keys_plane, keys_scales)
+        nc.sync.dma_start(out=q_raw[:], in_=query.rearrange("(p j) c -> p j c", j=PACK))
         nc.sync.dma_start(out=q2_raw[:], in_=query2.rearrange("(p j) c -> p j c", j=PACK))
-        nc.sync.dma_start(out=gout_raw[:], in_=gout.rearrange("(p j) c -> p j c", j=PACK))
         nc.sync.dma_start(out=w_raw[0][:], in_=w_rows[:, :, 0:HALF_COLS])
         load_scale_rows(nc.sync, tab_plane, tab_scales)
         nc.sync.dma_start(out=w_raw[1][:], in_=w_rows[:, :, HALF_COLS:R])
         nc.sync.dma_start(out=tab_pool[:].bitcast(I32), in_=tab_words[0].bitcast(I32))
+        nc.sync.dma_start(out=gain_sb[:], in_=gain.rearrange("(p t) o -> p (t o)", t=PACK))
+        nc.sync.dma_start(out=hsc_sb[:], in_=hsc.rearrange("(p t) o -> p (t o)", t=PACK))
+        nc.sync.dma_start(out=gout_raw[:], in_=gout.rearrange("(p j) c -> p j c", j=PACK))
         nc.sync.dma_start(out=total[:], in_=old)
-        nc.gpsimd.dma_start(out=gain_sb[:], in_=gain.rearrange("(p t) o -> p (t o)", t=PACK))
-        nc.gpsimd.dma_start(out=hsc_sb[:], in_=hsc.rearrange("(p t) o -> p (t o)", t=PACK))
-
-        nc.gpsimd.memset(placed[:], 0.0)
-        factor = sb.tile([P, PACK], F32, name="factor")
-        nc.gpsimd.tensor_tensor(factor[:], gain_sb[:], hsc_sb[:], ALU.mult)
 
         tab_bytes = sb.tile([P, I], U8, name="tab_bytes", align_bytes=64)
         keys_bytes = sb.tile([P, I], U8, name="keys_bytes", align_bytes=64)
@@ -82,36 +79,34 @@ def tile_attend_blrgained_asked_kernel(
         w_codes = sb.tile([P, PACK, P], U32, name="w_codes", align_bytes=64)
         w_bytes = sb.tile([P, PACK, P], U8, name="w_bytes", align_bytes=64)
 
+        w_grouped = sb.tile([P, PACK, P, PACK], BF16, name="w_grouped", align_bytes=64)
+
         def cast_w(h):
-            grouped = sb.tile([P, PACK, P // 2, PACK], BF16, name=f"w_grouped{h}", align_bytes=64)
             nc.scalar.activation(
-                grouped[:].rearrange("p t m j -> p m j t"),
+                w_grouped[:, :, h * P // 2 : (h + 1) * P // 2, :].rearrange("p t m j -> p m j t"),
                 w_raw[h][:].rearrange("p j (m t) -> p m j t", t=PACK),
                 ACT.Copy,
             )
-            return grouped
 
-        def quantize_w(h, grouped):
-            cols = slice(h * P // 2, (h + 1) * P // 2)
-            for t in range(PACK):
-                nc.vector.quantize_mx(
-                    out=w_codes[:, t, cols].bitcast(FP8X4),
-                    scales=w_bytes[:, t, cols],
-                    in_=grouped[:, t].rearrange("p m j -> p (m j)"),
-                )
+        def quantize_w(pair):
+            tiles = slice(2 * pair, 2 * pair + 2)
+            nc.vector.quantize_mx(
+                out=w_codes[:, tiles, :].rearrange("p t m -> p (t m)").bitcast(FP8X4),
+                scales=w_bytes[:, tiles, :].rearrange("p t m -> p (t m)"),
+                in_=w_grouped[:, tiles].rearrange("p t m j -> p (t m j)"),
+            )
 
-        def cast_cols(raw, name):
-            grouped = sb.tile([P, Q, PACK], BF16, name=name + "_grouped", align_bytes=64)
+        def cast_cols(raw, grouped):
             nc.scalar.activation(
-                grouped[:].rearrange("p (c i) j -> p c j i", i=4),
+                grouped.rearrange("p (c i) j -> p c j i", i=4),
                 raw[:].rearrange("p j (c i) -> p c j i", i=4),
                 ACT.Copy,
             )
-            return grouped
 
         def quantize_cols(grouped, name):
-            codes = sb.tile([P, Q], U32, name=name + "_codes", align_bytes=64)
-            scales = sb.tile([P, Q], U8, name=name + "_bytes", align_bytes=64)
+            width = grouped.shape[1]
+            codes = sb.tile([P, width], U32, name=name + "_codes", align_bytes=64)
+            scales = sb.tile([P, width], U8, name=name + "_bytes", align_bytes=64)
             nc.vector.quantize_mx(
                 out=codes[:].bitcast(FP8X4), scales=scales[:], in_=grouped[:].rearrange("p c j -> p (c j)")
             )
@@ -154,59 +149,63 @@ def tile_attend_blrgained_asked_kernel(
         def scores(bank, codes, scales):
             nc.tensor.matmul_mx(
                 out=bank[:],
-                lhsT=codes[:].bitcast(FP8X4),
-                lhsT_scale=scales[:],
+                lhsT=codes.bitcast(FP8X4),
+                lhsT_scale=scales,
                 rhs=keys_codes[:].bitcast(FP4X4),
                 rhs_scale=keys_bytes[:],
                 start=True,
                 stop=True,
             )
 
-        nc.vector.tensor_copy(keys_bytes[:], keys_plane[:].indirect(offsets[:]))
-        q_grouped = cast_cols(q_raw, "q")
-        q2_grouped = cast_cols(q2_raw, "q2")
-        gout_grouped = cast_cols(gout_raw, "gout")
+        both_grouped = sb.tile([P, 2 * Q, PACK], BF16, name="both_grouped", align_bytes=64)
+        gout_grouped = sb.tile([P, Q, PACK], BF16, name="gout_grouped", align_bytes=64)
+        cast_cols(q_raw, both_grouped[:, 0:Q, :])
+        cast_cols(q2_raw, both_grouped[:, Q : 2 * Q, :])
         nc.vector.tensor_copy(keys_codes[:], keys_pool[:].indirect(offsets[:]))
-        q_codes, q_bytes = quantize_cols(q_grouped, "q")
-        q2_codes, q2_bytes = quantize_cols(q2_grouped, "q2")
-        scores(a_ps, q_codes, q_bytes)
-        scores(b_ps, q2_codes, q2_bytes)
-        gout_codes, gout_bytes = quantize_cols(gout_grouped, "gout")
+        nc.vector.tensor_copy(keys_bytes[:], keys_plane[:].indirect(offsets[:]))
+        both_codes, both_bytes = quantize_cols(both_grouped, "both")
+        scores(a_ps, both_codes[:, 0:Q], both_bytes[:, 0:Q])
+        scores(b_ps, both_codes[:, Q : 2 * Q], both_bytes[:, Q : 2 * Q])
         nc.vector.tensor_copy(tab_bytes[:], tab_plane[:].indirect(offsets[:]))
 
-        w_grouped = [cast_w(h) for h in range(2)]
+        for h in range(2):
+            cast_w(h)
         neg_a = sb.tile([P, I], F32, name="neg_a")
         neg_max = sb.tile([P, 1], F32, name="neg_max")
         nc.vector.tensor_scalar(neg_a[:], a_ps[:], -1.0, None, ALU.mult, ALU.min, accum_out=neg_max[:])
-        quantize_w(0, w_grouped[0])
         logit = sb.tile([P, I], F32, name="logit")
         nc.vector.scalar_tensor_tensor(logit[:], b_ps[:], 0.0, neg_a[:], ALU.min, ALU.subtract)
         gather_tab(0)
-        quantize_w(1, w_grouped[1])
+        for pair in range(2):
+            quantize_w(pair)
         gather_tab(1)
+        factor = sb.tile([P, PACK], F32, name="factor")
+        nc.vector.tensor_tensor(factor[:], gain_sb[:], hsc_sb[:], ALU.mult)
         for c in range(n_chunks):
             layer(c)
 
-        half_abs = sb.tile([P, I], F32, name="half_abs", tag="w_raw1", align_bytes=64)
-        nc.scalar.activation(half_abs[:], b_ps[:], ACT.Abs, scale=0.5)
+        late = sb.tile([P, 2, I], F32, name="late", tag="w_raw1", align_bytes=64)
+        half_abs, expo = late[:, 0, :], late[:, 1, :]
+        nc.scalar.activation(half_abs, b_ps[:], ACT.Abs, scale=0.5)
         gate = sb.tile([P, I], F32, name="gate")
-        nc.scalar.activation(gate[:], half_abs[:], ACT.Tanh)
-        expo = sb.tile([P, I], F32, name="expo")
-        nc.scalar.activation(expo[:], logit[:], ACT.Exp, bias=neg_max[:])
+        nc.scalar.activation(gate[:], half_abs, ACT.Tanh)
+        nc.scalar.activation(expo, logit[:], ACT.Exp, bias=neg_max[:])
+        cast_cols(gout_raw, gout_grouped[:])
         ht = [squash(c) for c in range(n_chunks)]
 
         weight = sb.tile([P, I], F32, name="weight")
         row_sum = sb.tile([P, 1], F32, name="row_sum")
-        nc.vector.scalar_tensor_tensor(weight[:], gate[:], 1.0, expo[:], ALU.add, ALU.mult, accum_out=row_sum[:])
+        nc.vector.scalar_tensor_tensor(weight[:], gate[:], 1.0, expo, ALU.add, ALU.mult, accum_out=row_sum[:])
         hs = [scale_hidden(0, ht[0])]
         inv = sb.tile([P, 1], F32, name="inv")
         nc.vector.reciprocal(inv[:], row_sum[:])
         hs.append(scale_hidden(1, ht[1]))
         inv_scaled = sb.tile([P, 1], F32, name="inv_scaled")
-        nc.vector.tensor_scalar(inv_scaled[:], inv[:], 512.0, None, ALU.mult)
+        nc.scalar.activation(inv_scaled[:], inv[:], ACT.Copy, scale=512.0)
         neg_inv = sb.tile([P, 1], F32, name="neg_inv")
-        nc.vector.tensor_scalar(neg_inv[:], inv[:], -1.0, None, ALU.mult)
+        nc.scalar.activation(neg_inv[:], inv[:], ACT.Copy, scale=-1.0)
         hq = [quantize_cols(hs[0], "hs0")]
+        gout_codes, gout_bytes = quantize_cols(gout_grouped, "gout")
         for c in range(2, n_chunks):
             hs.append(scale_hidden(c, ht[c]))
             hq.append(quantize_cols(hs[c - 1], f"hs{c - 1}"))

from contextlib import ExitStack

import concourse.mybir as mybir

D, K, R, T, I, Q = 512, 512, 512, 2048, 512, 128
FLOPS = 2 * (2 * D * Q * I + K * R * I + R * Q * I)

F32 = mybir.dt.float32
BF16 = mybir.dt.bfloat16
I32 = mybir.dt.int32
U32 = mybir.dt.uint32
U16 = mybir.dt.uint16
U8 = mybir.dt.uint8
FP8X4 = mybir.dt.float8_e4m3fn_x4
FP4X4 = mybir.dt.float4_e2m1fn_x4
ALU = mybir.AluOpType
ACT = mybir.ActivationFunctionType

P = 128
PACK = 4
CHUNK = 128
HALF_COLS = R // 2
STORE_WIDTHS = (256, 512, 512, 512, 256)


def load_scale_rows(queue, plane, rows):
    for quad in range(4):
        queue.dma_start(
            out=plane[32 * quad : 32 * quad + 4, :].bitcast(I32),
            in_=rows[0, 4 * quad : 4 * quad + 4, :].bitcast(I32),
        )


def tile_attend_blrgained_asked_kernel(
    tc, query, query2, keys_words, keys_scales, tab_words, tab_scales, w1, gain, gout, hsc, old, offs, out
):
    nc = tc.nc
    with ExitStack() as ctx:
        sb = ctx.enter_context(tc.tile_pool(name="sb", bufs=1))
        ps = ctx.enter_context(tc.psum_pool(name="ps", bufs=1))

        offsets = sb.tile([P, I // 16], U16, name="offsets")
        tab_plane = sb.tile([P, T], U8, name="tab_plane", align_bytes=64)
        keys_plane = sb.tile([P, T], U8, name="keys_plane", align_bytes=64)
        tab_pool = sb.tile([P, T], U16, name="tab_pool", align_bytes=64)
        keys_pool = sb.tile([P, T], U16, name="keys_pool", align_bytes=64)
        placed = sb.tile([P, T], F32, name="placed", align_bytes=64)
        total = sb.tile([P, T], F32, name="total", align_bytes=64)
        w_raw = [sb.tile([P, PACK, HALF_COLS], F32, name=f"w_raw{h}", tag=f"w_raw{h}", align_bytes=64) for h in range(2)]
        q_raw = sb.tile([P, PACK, Q], F32, name="q_raw", align_bytes=64)
        q2_raw = sb.tile([P, PACK, Q], F32, name="q2_raw", align_bytes=64)
        gout_raw = sb.tile([P, PACK, Q], F32, name="gout_raw", align_bytes=64)
        gain_sb = sb.tile([P, PACK], F32, name="gain_sb")
        hsc_sb = sb.tile([P, PACK], F32, name="hsc_sb")

        nc.vector.memset(keys_plane[:].bitcast(I32), 0)
        nc.vector.memset(tab_plane[:].bitcast(I32), 0)
        nc.vector.memset(placed[:], 0.0)

        w_rows = w1.rearrange("(p j) c -> p j c", j=PACK)
        nc.sync.dma_start(offsets[:], offs)
        nc.sync.dma_start(out=keys_pool[:].bitcast(I32), in_=keys_words[0].bitcast(I32))
        load_scale_rows(nc.sync, keys_plane, keys_scales)
        nc.sync.dma_start(out=q_raw[:], in_=query.rearrange("(p j) c -> p j c", j=PACK))
        nc.sync.dma_start(out=q2_raw[:], in_=query2.rearrange("(p j) c -> p j c", j=PACK))
        nc.sync.dma_start(out=w_raw[0][:], in_=w_rows[:, :, 0:HALF_COLS])
        load_scale_rows(nc.sync, tab_plane, tab_scales)
        nc.sync.dma_start(out=w_raw[1][:], in_=w_rows[:, :, HALF_COLS:R])
        nc.sync.dma_start(out=tab_pool[:].bitcast(I32), in_=tab_words[0].bitcast(I32))
        nc.sync.dma_start(out=gain_sb[:], in_=gain.rearrange("(p t) o -> p (t o)", t=PACK))
        nc.sync.dma_start(out=hsc_sb[:], in_=hsc.rearrange("(p t) o -> p (t o)", t=PACK))
        nc.sync.dma_start(out=gout_raw[:], in_=gout.rearrange("(p j) c -> p j c", j=PACK))
        nc.sync.dma_start(out=total[:], in_=old)

        tab_bytes = sb.tile([P, I], U8, name="tab_bytes", align_bytes=64)
        keys_bytes = sb.tile([P, I], U8, name="keys_bytes", align_bytes=64)
        tab_codes = sb.tile([P, I], U16, name="tab_codes", align_bytes=64)
        keys_codes = sb.tile([P, I], U16, name="keys_codes", align_bytes=64)
        w_codes = sb.tile([P, PACK, P], U32, name="w_codes", align_bytes=64)
        w_bytes = sb.tile([P, PACK, P], U8, name="w_bytes", align_bytes=64)

        w_grouped = sb.tile([P, PACK, P, PACK], BF16, name="w_grouped", align_bytes=64)

        def cast_w(h):
            nc.scalar.activation(
                w_grouped[:, :, h * P // 2 : (h + 1) * P // 2, :].rearrange("p t m j -> p m j t"),
                w_raw[h][:].rearrange("p j (m t) -> p m j t", t=PACK),
                ACT.Copy,
            )

        def quantize_w(pair):
            tiles = slice(2 * pair, 2 * pair + 2)
            nc.vector.quantize_mx(
                out=w_codes[:, tiles, :].rearrange("p t m -> p (t m)").bitcast(FP8X4),
                scales=w_bytes[:, tiles, :].rearrange("p t m -> p (t m)"),
                in_=w_grouped[:, tiles].rearrange("p t m j -> p (t m j)"),
            )

        def cast_cols(raw, grouped):
            nc.scalar.activation(
                grouped.rearrange("p (c i) j -> p c j i", i=4),
                raw[:].rearrange("p j (c i) -> p c j i", i=4),
                ACT.Copy,
            )

        def quantize_cols(grouped, name):
            width = grouped.shape[1]
            codes = sb.tile([P, width], U32, name=name + "_codes", align_bytes=64)
            scales = sb.tile([P, width], U8, name=name + "_bytes", align_bytes=64)
            nc.vector.quantize_mx(
                out=codes[:].bitcast(FP8X4), scales=scales[:], in_=grouped[:].rearrange("p c j -> p (c j)")
            )
            return codes, scales

        n_chunks = I // CHUNK
        zh = [ps.tile([P, PACK, CHUNK], F32, name=f"zh{c}") for c in range(n_chunks)]
        a_ps = ps.tile([P, I], F32, name="a_ps")
        b_ps = ps.tile([P, I], F32, name="b_ps")
        c0_ps = ps.tile([P, I], F32, name="c0_ps")

        def gather_tab(h):
            nc.vector.tensor_copy(
                tab_codes[:, h * I // 2 : (h + 1) * I // 2], tab_pool[:].indirect(offsets[:, h * 16 : (h + 1) * 16])
            )

        def layer(c):
            cols = slice(c * CHUNK, (c + 1) * CHUNK)
            for t in range(PACK):
                nc.tensor.matmul_mx(
                    out=zh[c][:, t, :],
                    lhsT=w_codes[:, t, :].bitcast(FP8X4),
                    lhsT_scale=w_bytes[:, t, :],
                    rhs=tab_codes[:, cols].bitcast(FP4X4),
                    rhs_scale=tab_bytes[:, cols],
                    start=True,
                    stop=True,
                )

        def squash(c):
            ht = sb.tile([P, CHUNK, PACK], F32, name=f"ht{c}", align_bytes=64)
            nc.scalar.activation(ht[:], zh[c][:].rearrange("p t n -> p n t"), ACT.Tanh)
            return ht

        def scale_hidden(c, ht):
            hs = sb.tile([P, CHUNK, PACK], BF16, name=f"hs{c}_grouped", align_bytes=64)
            nc.vector.tensor_tensor(hs[:], ht[:], factor[:].unsqueeze(1).to_broadcast([P, CHUNK, PACK]), ALU.mult)
            return hs

        def scores(bank, codes, scales):
            nc.tensor.matmul_mx(
                out=bank[:],
                lhsT=codes.bitcast(FP8X4),
                lhsT_scale=scales,
                rhs=keys_codes[:].bitcast(FP4X4),
                rhs_scale=keys_bytes[:],
                start=True,
                stop=True,
            )

        both_grouped = sb.tile([P, 2 * Q, PACK], BF16, name="both_grouped", align_bytes=64)
        gout_grouped = sb.tile([P, Q, PACK], BF16, name="gout_grouped", align_bytes=64)
        cast_cols(q_raw, both_grouped[:, 0:Q, :])
        cast_cols(q2_raw, both_grouped[:, Q : 2 * Q, :])
        nc.vector.tensor_copy(keys_codes[:], keys_pool[:].indirect(offsets[:]))
        nc.vector.tensor_copy(keys_bytes[:], keys_plane[:].indirect(offsets[:]))
        both_codes, both_bytes = quantize_cols(both_grouped, "both")
        scores(a_ps, both_codes[:, 0:Q], both_bytes[:, 0:Q])
        scores(b_ps, both_codes[:, Q : 2 * Q], both_bytes[:, Q : 2 * Q])
        nc.vector.tensor_copy(tab_bytes[:], tab_plane[:].indirect(offsets[:]))

        for h in range(2):
            cast_w(h)
        neg_a = sb.tile([P, I], F32, name="neg_a")
        neg_max = sb.tile([P, 1], F32, name="neg_max")
        nc.vector.tensor_scalar(neg_a[:], a_ps[:], -1.0, None, ALU.mult, ALU.min, accum_out=neg_max[:])
        logit = sb.tile([P, I], F32, name="logit")
        nc.vector.scalar_tensor_tensor(logit[:], b_ps[:], 0.0, neg_a[:], ALU.min, ALU.subtract)
        gather_tab(0)
        for pair in range(2):
            quantize_w(pair)
        gather_tab(1)
        factor = sb.tile([P, PACK], F32, name="factor")
        nc.vector.tensor_tensor(factor[:], gain_sb[:], hsc_sb[:], ALU.mult)
        for c in range(n_chunks):
            layer(c)

        late = sb.tile([P, 2, I], F32, name="late", tag="w_raw1", align_bytes=64)
        half_abs, expo = late[:, 0, :], late[:, 1, :]
        nc.scalar.activation(half_abs, b_ps[:], ACT.Abs, scale=0.5)
        gate = sb.tile([P, I], F32, name="gate")
        nc.scalar.activation(gate[:], half_abs, ACT.Tanh)
        nc.scalar.activation(expo, logit[:], ACT.Exp, bias=neg_max[:])
        cast_cols(gout_raw, gout_grouped[:])
        ht = [squash(c) for c in range(n_chunks)]

        weight = sb.tile([P, I], F32, name="weight")
        row_sum = sb.tile([P, 1], F32, name="row_sum")
        nc.vector.scalar_tensor_tensor(weight[:], gate[:], 1.0, expo, ALU.add, ALU.mult, accum_out=row_sum[:])
        hs = [scale_hidden(0, ht[0])]
        inv = sb.tile([P, 1], F32, name="inv")
        nc.vector.reciprocal(inv[:], row_sum[:])
        hs.append(scale_hidden(1, ht[1]))
        inv_scaled = sb.tile([P, 1], F32, name="inv_scaled")
        nc.scalar.activation(inv_scaled[:], inv[:], ACT.Copy, scale=512.0)
        neg_inv = sb.tile([P, 1], F32, name="neg_inv")
        nc.scalar.activation(neg_inv[:], inv[:], ACT.Copy, scale=-1.0)
        hq = [quantize_cols(hs[0], "hs0")]
        gout_codes, gout_bytes = quantize_cols(gout_grouped, "gout")
        for c in range(2, n_chunks):
            hs.append(scale_hidden(c, ht[c]))
            hq.append(quantize_cols(hs[c - 1], f"hs{c - 1}"))
        hq.append(quantize_cols(hs[-1], f"hs{n_chunks - 1}"))

        for c in range(n_chunks):
            nc.tensor.matmul_mx(
                out=c0_ps[:, c * CHUNK : (c + 1) * CHUNK],
                lhsT=gout_codes[:].bitcast(FP8X4),
                lhsT_scale=gout_bytes[:],
                rhs=hq[c][0][:].bitcast(FP8X4),
                rhs_scale=hq[c][1][:],
                start=True,
                stop=True,
            )

        direct = sb.tile([P, I], F32, name="direct")
        direct_sum = sb.tile([P, 1], F32, name="direct_sum")
        nc.vector.scalar_tensor_tensor(
            direct[:], c0_ps[:], inv_scaled[:], weight[:], ALU.mult, ALU.mult, accum_out=direct_sum[:]
        )
        through = sb.tile([P, I], F32, name="through")
        nc.vector.tensor_scalar(through[:], weight[:], direct_sum[:], neg_inv[:], ALU.mult, ALU.mult)
        nc.vector.tensor_tensor(placed[:].indirect(offsets[:]), direct[:], through[:], ALU.add)

        start = 0
        for width in STORE_WIDTHS:
            cols = slice(start, start + width)
            nc.vector.tensor_tensor(total[:, cols], placed[:, cols], total[:, cols], ALU.add)
            nc.sync.dma_start(out=out[:, cols], in_=total[:, cols])
            start = start + width
